import numpy as np, ml_dtypes
CORES = [15,47,79,175,207]
N = 5
import mx_ref
NC = 128
BF = ml_dtypes.bfloat16
def cut(t, i, w=512):
    return t[:, w * i:w * i + w]
def term(a, B):
    return np.stack([np.maximum(mx_ref.matmul(mx_ref.quantize(cut(a, i)), B), 0) for i in range(4)], axis=2).reshape(128, -1)
def setup_inputs(rng):
    def f(*shape):
        return mx_ref.flush((rng.standard_normal(shape, dtype=np.float32) * np.exp2(rng.integers(-2, 3, shape[:-1] + (1,)))).astype(BF))
    return {"a": f(N, 128, 4 * 512), "b": f(N, 128, 4 * NC)}
def setup_inputs_blocks(rng):
    d = setup_inputs(rng)
    for k in ("a", "b"): d[k] = mx_ref.spread(d[k], rng, 2)
    return d
def setup_inputs_wide(rng):
    d = setup_inputs(rng)
    for k in ("a", "b"): d[k] = mx_ref.flush((d[k].astype(np.float32) * np.exp2(rng.integers(-4, 5, (N, 1, 1))).astype(np.float32)).astype(BF))
    return d
def setup_inputs_lossless(rng):
    a = np.zeros((N, 128, 4 * 128, 4), np.float32)
    for r in range(N):
        k = rng.integers(0, 512, size=4 * 128)
        a[r, k // 4, np.arange(4 * 128), k % 4] = 1.0
    size = np.repeat(2.0 ** rng.integers(-4, 5, size=(1, 1, (4 * NC) // 4)), 4, axis=2)
    b = (rng.random((N, 128, 4 * NC)) < 0.8) * size
    return {"a": a.reshape(N, 128, 4 * 512).astype(BF), "b": b.astype(np.float32).astype(BF)}
def reference(a, b):
    Bq = [mx_ref.quantize(b[c]) for c in range(N)]
    y = np.zeros((N, 128, 4 * NC), np.float32)
    for c in range(N):
        y[c] = mx_ref.total([term(a[r], Bq[c]) for r in range(N)])
    return {"y": y}

@@ -1,0 +1,177 @@
+from concourse.bass import DstId, RemoteDMATransfer
+from concourse.mybir import dt, AluOpType, ActivationFunctionType
+
+NR = 5
+W = 128
+TILE = 4 * W
+WORKER = {0: 0, 1: 0, 2: 0, 3: 1, 4: 1}
+
+SCRATCH = {
+    "bt": ("sbuf", [128, TILE], "bfloat16"),
+    "at": ("sbuf", [128, 4 * TILE], "bfloat16"),
+    "bq": ("sbuf", [128, NR * W], "float8_e4m3fn_x4"),
+    "bs": ("sbuf", [128, NR * W], "uint8"),
+    "aq": ("sbuf", [128, 4 * W], "float8_e4m3fn_x4"),
+    "asc": ("sbuf", [128, 4 * W], "uint8"),
+    "h": ("sbuf", [128, NR * TILE], "bfloat16"),
+    "hq": ("sbuf", [128, NR * W], "float8_e4m3fn_x4"),
+    "hs": ("sbuf", [128, NR * W], "uint8"),
+    "tq": ("sbuf", [128, NR * W], "float8_e4m3fn_x4"),
+    "ts": ("sbuf", [128, NR * W], "uint8"),
+    "one": ("sbuf", [128, TILE + 4], "bfloat16"),
+    "z": ("sbuf", [128, TILE + 4], "bfloat16"),
+    "wq": ("sbuf", [128, 4 * W], "float8_e4m3fn_x4"),
+    "wsc": ("sbuf", [128, 4 * W], "uint8"),
+    "ysb": ("sbuf", [128, TILE], "float32"),
+    "pt": ("psum", [128, 2048], "float32"),
+    "py": ("psum", [128, 2048], "float32"),
+}
+SEMAPHORES = (["ldb", "lda0", "lda1", "vb", "va", "mm", "rs", "rv", "vh", "my", "ys", "yv", "stored", "sent", "aarr", "warr",
+               "vm", "gz", "vw"] + ["b%d" % i for i in range(NR)] + ["t%d" % i for i in range(NR)])
+
+
+def _bits(mask):
+    return [e for e in range(16) if mask >> e & 1]
+
+
+def _part(mask, k, n):
+    b = _bits(mask)
+    m = len(b) // n
+    return sum(1 << e for e in b[k * m:(k + 1) * m])
+
+
+def _workers(T, topo, r):
+    home = T.cores[r]
+    far = [c for c in range(max(0, home - 8), home + 9)
+           if topo.host(c) == topo.host(home) and topo.chip(c) == topo.chip(home) and topo.die(c) != topo.die(home)]
+    return [home, far[-1]]
+
+
+def rank_program(g, core, T, topo):
+    S = T.sem
+    u8 = dt.uint8
+    crew = [_workers(T, topo, r) for r in range(NR)]
+    mine = [r for r in range(NR) if core in crew[r]]
+    if not mine:
+        return
+    r = mine[0]
+    home, helper = crew[r]
+    at_home = core == home
+    jobs = [(r + d) % NR for d in range(1, NR) if WORKER[d] == crew[r].index(core)]
+    off = topo.mask(core, T.cores[(r + 1) % NR])
+    near = topo.mask(core, helper if at_home else home)
+    chip_only = near & ~off
+
+    def cols(k, n=1):
+        return slice(k * W, (k + n) * W)
+
+    def dst(d):
+        rid, pid = topo.addr(d, core)
+        return DstId(rid=rid, pnc=pid)
+
+    sent = [0]
+
+    def fused(items):
+        g.remote_dma_fused([RemoteDMATransfer(srcs=[s], dsts=ds, dst_ids=[dst(d) for d in cs], dma_engine_mask=m, remote_sem=sem)
+                            for s, ds, cs, m, sem in items], local_sem=S.sent)
+        sent[0] += sum(len(_bits(m)) for _, _, _, m, _ in items)
+
+    def send(view, to, mask, sem):
+        rid, pid = topo.addr(to, core)
+        g.remote_dma(view, view, sem, S.sent, pid, rid, mask)
+        sent[0] += len(_bits(mask))
+
+    if at_home:
+        g.sync.dma_start(T.bt[:], T.b[:]).then_inc(S.ldb, 16)
+        for k in range(2):
+            p = slice(k * 2 * TILE, (k + 1) * 2 * TILE)
+            g.sync.dma_start(T.at[:, p], T.a[:, p]).then_inc(S["lda%d" % k], 16)
+        g.vector.wait_ge(S.ldb, 16)
+        g.vector.quantize_mx(T.bq[:, cols(r)], T.bs[:, cols(r)], T.bt[:]).then_inc(S.vb, 1)
+        for k in range(2):
+            g.vector.wait_ge(S["lda%d" % k], 16)
+            g.vector.quantize_mx(T.aq[:, cols(2 * k, 2)], T.asc[:, cols(2 * k, 2)],
+                                 T.at[:, k * 2 * TILE:(k + 1) * 2 * TILE]).then_inc(S.va, 1)
+        to = [crew[(r - d) % NR][WORKER[d]] for d in range(1, NR)]
+        g.wait_ge(S.vb, 1)
+        cq = T.bq[:, cols(r)].bitcast(u8)
+        cs = T.bs[:, cols(r)]
+        fused([(cq, [cq] * len(to), to, off, S["b%d" % r])])
+        fused([(cs, [cs] * len(to), to, off, S["b%d" % r])])
+        g.wait_ge(S.va, 2)
+        send(T.aq[:].bitcast(u8), helper, chip_only, S.aarr)
+        send(T.asc[:], helper, chip_only, S.aarr)
+    else:
+        g.vector.memset(T.one[:], 1.0).then_inc(S.vm, 1)
+        g.wait_ge(S.vm, 1)
+        g.affine_select(T.z[:], T.one[:], [[1, TILE + 4]], AluOpType.is_equal, 0.0, -3, -4).then_inc(S.gz, 1)
+        g.vector.wait_ge(S.gz, 1)
+        for i in range(4):
+            g.vector.quantize_mx(T.wq[:, cols(i)], T.wsc[:, cols(i)], T.z[:, 3 - i:3 - i + TILE]).then_inc(S.vw, 1)
+        g.wait_ge(S.vw, 4)
+        send(T.wq[:].bitcast(u8), home, off, S.warr)
+        send(T.wsc[:], home, off, S.warr)
+
+    todo = ([r] if at_home else []) + jobs
+    if not at_home:
+        g.tensor.wait_ge(S.aarr, 2 * len(_bits(chip_only)))
+    for k, c in enumerate(todo):
+        if c == r:
+            g.tensor.wait_ge(S.vb, 1)
+        else:
+            g.tensor.wait_ge(S["b%d" % c], 2 * len(_bits(off)))
+        for i in range(4):
+            if c == r and i % 2 == 0:
+                g.tensor.wait_ge(S.va, 1 + i // 2)
+            if k:
+                g.tensor.wait_ge(S.rs if i % 2 == 0 else S.rv, 2 * (k - 1) + 1 + i // 2)
+            g.tensor.matmul_mx(T.pt[:, 512 * i:512 * i + W], T.aq[:, cols(i)], T.asc[:, cols(i)],
+                               T.bq[:, cols(c)], T.bs[:, cols(c)], True, True).then_inc(S.mm, 1)
+        for i in range(4):
+            o = T.h[:, c * TILE + i:(c + 1) * TILE:4]
+            p = T.pt[:, 512 * i:512 * i + W]
+            q = g.scalar if i % 2 == 0 else g.vector
+            q.wait_ge(S.mm, 4 * k + i + 1)
+            if i % 2 == 0:
+                g.scalar.activation(o, p, ActivationFunctionType.Relu).then_inc(S.rs, 1)
+            else:
+                g.vector.tensor_scalar(o, p, 0.0, None, AluOpType.max).then_inc(S.rv, 1)
+        g.vector.wait_ge(S.rs, 2 * (k + 1))
+        g.vector.wait_ge(S.rv, 2 * (k + 1))
+        g.vector.quantize_mx(T.hq[:, cols(c)], T.hs[:, cols(c)], T.h[:, c * TILE:(c + 1) * TILE]).then_inc(S.vh, 1)
+    g.wait_ge(S.vh, len(todo))
+    n = len(jobs)
+    fused([(T.hq[:, cols(c)].bitcast(u8), [T.tq[:, cols(r)].bitcast(u8)], [T.cores[c]], _part(off, k, n), S["t%d" % r])
+           for k, c in enumerate(jobs)])
+    fused([(T.hs[:, cols(c)], [T.ts[:, cols(r)]], [T.cores[c]], _part(off, k, n), S["t%d" % r])
+           for k, c in enumerate(jobs)])
+
+    if at_home:
+        order = [(r - d) % NR for d in range(NR)]
+        g.tensor.wait_ge(S.warr, 2 * len(_bits(off)))
+        for k, s in enumerate(order):
+            if s == r:
+                g.tensor.wait_ge(S.vh, 1)
+                x, xs = T.hq[:, cols(r)], T.hs[:, cols(r)]
+            else:
+                share = len(_bits(off)) // sum(1 for d in range(1, NR) if WORKER[d] == WORKER[(r - s) % NR])
+                g.tensor.wait_ge(S["t%d" % s], 2 * share)
+                x, xs = T.tq[:, cols(s)], T.ts[:, cols(s)]
+            last = k == NR - 1
+            for i in range(4):
+                m = g.tensor.matmul_mx(T.py[:, 512 * i:512 * i + W], T.wq[:, cols(i)], T.wsc[:, cols(i)], x, xs, k == 0, last)
+                if last:
+                    m.then_inc(S.my, 1)
+        for i in range(4):
+            o, p = T.ysb[:, i:TILE:4], T.py[:, 512 * i:512 * i + W]
+            if i % 2 == 0:
+                g.scalar.wait_ge(S.my, i + 1)
+                g.scalar.activation(o, p, ActivationFunctionType.Copy).then_inc(S.ys, 1)
+            else:
+                g.vector.wait_ge(S.my, i + 1)
+                g.vector.tensor_copy(o, p).then_inc(S.yv, 1)
+        g.sync.wait_ge(S.ys, 2)
+        g.sync.wait_ge(S.yv, 2)
+        g.sync.dma_start(T.y[:], T.ysb[:]).then_inc(S.stored, 16)
+        g.sync.wait_ge(S.stored, 16)
+    g.wait_ge(S.sent, sent[0])

@@ -4,6 +4,7 @@ from concourse.mybir import dt, AluOpType, ActivationFunctionType
 NR = 5
 W = 128
 TILE = 4 * W
+WAVES = ((1, 3), (2, 4))
 WORKER = {0: 0, 1: 0, 2: 0, 3: 1, 4: 1}
 
 SCRATCH = {
@@ -34,12 +35,6 @@ def _bits(mask):
     return [e for e in range(16) if mask >> e & 1]
 
 
-def _part(mask, k, n):
-    b = _bits(mask)
-    m = len(b) // n
-    return sum(1 << e for e in b[k * m:(k + 1) * m])
-
-
 def _workers(T, topo, r):
     home = T.cores[r]
     far = [c for c in range(max(0, home - 8), home + 9)
@@ -57,28 +52,27 @@ def rank_program(g, core, T, topo):
     r = mine[0]
     home, helper = crew[r]
     at_home = core == home
-    jobs = [(r + d) % NR for d in range(1, NR) if WORKER[d] == crew[r].index(core)]
+    jobs = [(r + d) % NR for wave in WAVES for d in wave if WORKER[d] == crew[r].index(core)]
     off = topo.mask(core, T.cores[(r + 1) % NR])
-    near = topo.mask(core, helper if at_home else home)
-    chip_only = near & ~off
+    chip_only = topo.mask(core, helper if at_home else home) & ~off
 
     def cols(k, n=1):
         return slice(k * W, (k + n) * W)
 
-    def dst(d):
-        rid, pid = topo.addr(d, core)
-        return DstId(rid=rid, pnc=pid)
-
     sent = [0]
 
-    def fused(items):
-        g.remote_dma_fused([RemoteDMATransfer(srcs=[s], dsts=ds, dst_ids=[dst(d) for d in cs], dma_engine_mask=m, remote_sem=sem)
-                            for s, ds, cs, m, sem in items], local_sem=S.sent)
-        sent[0] += sum(len(_bits(m)) for _, _, _, m, _ in items)
+    def multicast(view, to, mask, sem):
+        ids = []
+        for d in to:
+            rid, pid = topo.addr(d, core)
+            ids.append(DstId(rid=rid, pnc=pid))
+        g.remote_dma_fused([RemoteDMATransfer(srcs=[view], dsts=[view] * len(to), dst_ids=ids, dma_engine_mask=mask,
+                                              remote_sem=sem)], local_sem=S.sent)
+        sent[0] += len(_bits(mask))
 
-    def send(view, to, mask, sem):
+    def send(out, view, to, mask, sem):
         rid, pid = topo.addr(to, core)
-        g.remote_dma(view, view, sem, S.sent, pid, rid, mask)
+        g.remote_dma(out, view, sem, S.sent, pid, rid, mask)
         sent[0] += len(_bits(mask))
 
     if at_home:
@@ -92,15 +86,16 @@ def rank_program(g, core, T, topo):
             g.vector.wait_ge(S["lda%d" % k], 16)
             g.vector.quantize_mx(T.aq[:, cols(2 * k, 2)], T.asc[:, cols(2 * k, 2)],
                                  T.at[:, k * 2 * TILE:(k + 1) * 2 * TILE]).then_inc(S.va, 1)
-        to = [crew[(r - d) % NR][WORKER[d]] for d in range(1, NR)]
         g.wait_ge(S.vb, 1)
-        cq = T.bq[:, cols(r)].bitcast(u8)
-        cs = T.bs[:, cols(r)]
-        fused([(cq, [cq] * len(to), to, off, S["b%d" % r])])
-        fused([(cs, [cs] * len(to), to, off, S["b%d" % r])])
-        g.wait_ge(S.va, 2)
-        send(T.aq[:].bitcast(u8), helper, chip_only, S.aarr)
-        send(T.asc[:], helper, chip_only, S.aarr)
+        for wave in WAVES:
+            to = [crew[(r - d) % NR][WORKER[d]] for d in wave]
+            multicast(T.bq[:, cols(r)].bitcast(u8), to, off, S["b%d" % r])
+            multicast(T.bs[:, cols(r)], to, off, S["b%d" % r])
+        for k in range(2):
+            g.wait_ge(S.va, k + 1)
+            v = T.aq[:, cols(2 * k, 2)].bitcast(u8)
+            send(v, v, helper, chip_only, S.aarr)
+        send(T.asc[:], T.asc[:], helper, chip_only, S.aarr)
     else:
         g.vector.memset(T.one[:], 1.0).then_inc(S.vm, 1)
         g.wait_ge(S.vm, 1)
@@ -109,12 +104,13 @@ def rank_program(g, core, T, topo):
         for i in range(4):
             g.vector.quantize_mx(T.wq[:, cols(i)], T.wsc[:, cols(i)], T.z[:, 3 - i:3 - i + TILE]).then_inc(S.vw, 1)
         g.wait_ge(S.vw, 4)
-        send(T.wq[:].bitcast(u8), home, off, S.warr)
-        send(T.wsc[:], home, off, S.warr)
+        v = T.wq[:].bitcast(u8)
+        send(v, v, home, off, S.warr)
+        send(T.wsc[:], T.wsc[:], home, off, S.warr)
 
     todo = ([r] if at_home else []) + jobs
     if not at_home:
-        g.tensor.wait_ge(S.aarr, 2 * len(_bits(chip_only)))
+        g.tensor.wait_ge(S.aarr, 3 * len(_bits(chip_only)))
     for k, c in enumerate(todo):
         if c == r:
             g.tensor.wait_ge(S.vb, 1)
@@ -139,23 +135,20 @@ def rank_program(g, core, T, topo):
         g.vector.wait_ge(S.rs, 2 * (k + 1))
         g.vector.wait_ge(S.rv, 2 * (k + 1))
         g.vector.quantize_mx(T.hq[:, cols(c)], T.hs[:, cols(c)], T.h[:, c * TILE:(c + 1) * TILE]).then_inc(S.vh, 1)
-    g.wait_ge(S.vh, len(todo))
-    n = len(jobs)
-    fused([(T.hq[:, cols(c)].bitcast(u8), [T.tq[:, cols(r)].bitcast(u8)], [T.cores[c]], _part(off, k, n), S["t%d" % r])
-           for k, c in enumerate(jobs)])
-    fused([(T.hs[:, cols(c)], [T.ts[:, cols(r)]], [T.cores[c]], _part(off, k, n), S["t%d" % r])
-           for k, c in enumerate(jobs)])
+        if c != r:
+            g.wait_ge(S.vh, k + 1)
+            send(T.tq[:, cols(r)].bitcast(u8), T.hq[:, cols(c)].bitcast(u8), T.cores[c], off, S["t%d" % r])
+            send(T.ts[:, cols(r)], T.hs[:, cols(c)], T.cores[c], off, S["t%d" % r])
 
     if at_home:
-        order = [(r - d) % NR for d in range(NR)]
+        order = [r] + [(r - d) % NR for wave in WAVES for d in wave]
         g.tensor.wait_ge(S.warr, 2 * len(_bits(off)))
         for k, s in enumerate(order):
             if s == r:
                 g.tensor.wait_ge(S.vh, 1)
                 x, xs = T.hq[:, cols(r)], T.hs[:, cols(r)]
             else:
-                share = len(_bits(off)) // sum(1 for d in range(1, NR) if WORKER[d] == WORKER[(r - s) % NR])
-                g.tensor.wait_ge(S["t%d" % s], 2 * share)
+                g.tensor.wait_ge(S["t%d" % s], 2 * len(_bits(off)))
                 x, xs = T.tq[:, cols(s)], T.ts[:, cols(s)]
             last = k == NR - 1
             for i in range(4):

@@ -4,8 +4,8 @@ from concourse.mybir import dt, AluOpType, ActivationFunctionType
 NR = 5
 W = 128
 TILE = 4 * W
-WAVES = ((1, 3), (2, 4))
-WORKER = {0: 0, 1: 0, 2: 0, 3: 1, 4: 1}
+HALF = 2 * TILE
+DIRECT, RELAYED = (1, 2, 3), 4
 
 SCRATCH = {
     "bt": ("sbuf", [128, TILE], "bfloat16"),
@@ -19,16 +19,15 @@ SCRATCH = {
     "hs": ("sbuf", [128, NR * W], "uint8"),
     "tq": ("sbuf", [128, NR * W], "float8_e4m3fn_x4"),
     "ts": ("sbuf", [128, NR * W], "uint8"),
-    "one": ("sbuf", [128, TILE + 4], "bfloat16"),
-    "z": ("sbuf", [128, TILE + 4], "bfloat16"),
+    "z": ("sbuf", [128, HALF], "bfloat16"),
     "wq": ("sbuf", [128, 4 * W], "float8_e4m3fn_x4"),
     "wsc": ("sbuf", [128, 4 * W], "uint8"),
     "ysb": ("sbuf", [128, TILE], "float32"),
     "pt": ("psum", [128, 2048], "float32"),
     "py": ("psum", [128, 2048], "float32"),
 }
-SEMAPHORES = (["ldb", "lda0", "lda1", "vb", "va", "mm", "rs", "rv", "vh", "my", "ys", "yv", "stored", "sent", "aarr", "warr",
-               "vm", "gz", "vw"] + ["b%d" % i for i in range(NR)] + ["t%d" % i for i in range(NR)])
+SEMAPHORES = (["ldb", "lda0", "lda1", "vb", "va", "mm", "rs", "rv", "vh", "my", "ys", "yv", "st0", "st1", "sent", "aarr0",
+               "aarr1", "warr", "vm", "gz", "vw"] + ["b%d" % i for i in range(NR)] + ["t%d" % i for i in range(NR)])
 
 
 def _bits(mask):
@@ -39,7 +38,7 @@ def _workers(T, topo, r):
     home = T.cores[r]
     far = [c for c in range(max(0, home - 8), home + 9)
            if topo.host(c) == topo.host(home) and topo.chip(c) == topo.chip(home) and topo.die(c) != topo.die(home)]
-    return [home, far[-1]]
+    return [home, far[-1], far[0]]
 
 
 def rank_program(g, core, T, topo):
@@ -50,9 +49,8 @@ def rank_program(g, core, T, topo):
     if not mine:
         return
     r = mine[0]
-    home, helper = crew[r]
+    home, helper, maker = crew[r]
     at_home = core == home
-    jobs = [(r + d) % NR for wave in WAVES for d in wave if WORKER[d] == crew[r].index(core)]
     off = topo.mask(core, T.cores[(r + 1) % NR])
     chip_only = topo.mask(core, helper if at_home else home) & ~off
 
@@ -61,20 +59,32 @@ def rank_program(g, core, T, topo):
 
     sent = [0]
 
-    def multicast(view, to, mask, sem):
-        ids = []
-        for d in to:
-            rid, pid = topo.addr(d, core)
-            ids.append(DstId(rid=rid, pnc=pid))
-        g.remote_dma_fused([RemoteDMATransfer(srcs=[view], dsts=[view] * len(to), dst_ids=ids, dma_engine_mask=mask,
-                                              remote_sem=sem)], local_sem=S.sent)
-        sent[0] += len(_bits(mask))
-
     def send(out, view, to, mask, sem):
         rid, pid = topo.addr(to, core)
         g.remote_dma(out, view, sem, S.sent, pid, rid, mask)
         sent[0] += len(_bits(mask))
 
+    def identity(half):
+        p = slice(64 * half, 64 * half + 64)
+        g.vector.memset(T.z[:], 0.0).then_inc(S.vm, 1)
+        g.wait_ge(S.vm, 1)
+        for t in range(4):
+            v = T.z[p, 5 * t:HALF:16]
+            g.affine_select(v, v, [[1, 64]], AluOpType.not_equal, 1.0, 0, -1).then_inc(S.gz, 1)
+        g.vector.wait_ge(S.gz, 4)
+        w = cols(2 * half, 2)
+        g.vector.quantize_mx(T.wq[:, w], T.wsc[:, w], T.z[:]).then_inc(S.vw, 1)
+        g.wait_ge(S.vw, 1)
+        send(T.wq[:, w].bitcast(u8), T.wq[:, w].bitcast(u8), home, off, S.warr)
+        send(T.wsc[:, w], T.wsc[:, w], home, off, S.warr)
+
+    if core == maker:
+        identity(1)
+        g.wait_ge(S.sent, sent[0])
+        return
+
+    mycodes, myscales = T.bq[:, cols(r)].bitcast(u8), T.bs[:, cols(r)]
+    fourth = crew[(r - RELAYED) % NR][1]
     if at_home:
         g.sync.dma_start(T.bt[:], T.b[:]).then_inc(S.ldb, 16)
         for k in range(2):
@@ -87,42 +97,42 @@ def rank_program(g, core, T, topo):
             g.vector.quantize_mx(T.aq[:, cols(2 * k, 2)], T.asc[:, cols(2 * k, 2)],
                                  T.at[:, k * 2 * TILE:(k + 1) * 2 * TILE]).then_inc(S.va, 1)
         g.wait_ge(S.vb, 1)
-        for wave in WAVES:
-            to = [crew[(r - d) % NR][WORKER[d]] for d in wave]
-            multicast(T.bq[:, cols(r)].bitcast(u8), to, off, S["b%d" % r])
-            multicast(T.bs[:, cols(r)], to, off, S["b%d" % r])
+        for k, d in enumerate(DIRECT):
+            send(mycodes, mycodes, T.cores[(r - d) % NR], off, S["b%d" % r])
+            if k == 0:
+                send(mycodes, mycodes, helper, chip_only, S["b%d" % r])
+            send(myscales, myscales, T.cores[(r - d) % NR], off, S["b%d" % r])
+        send(myscales, myscales, fourth, off, S["b%d" % r])
         for k in range(2):
             g.wait_ge(S.va, k + 1)
             v = T.aq[:, cols(2 * k, 2)].bitcast(u8)
-            send(v, v, helper, chip_only, S.aarr)
-        send(T.asc[:], T.asc[:], helper, chip_only, S.aarr)
+            send(v, v, helper, chip_only, S["aarr%d" % k])
+            v = T.asc[:, cols(2 * k, 2)]
+            send(v, v, helper, chip_only, S["aarr%d" % k])
     else:
-        g.vector.memset(T.one[:], 1.0).then_inc(S.vm, 1)
-        g.wait_ge(S.vm, 1)
-        g.affine_select(T.z[:], T.one[:], [[1, TILE + 4]], AluOpType.is_equal, 0.0, -3, -4).then_inc(S.gz, 1)
-        g.vector.wait_ge(S.gz, 1)
-        for i in range(4):
-            g.vector.quantize_mx(T.wq[:, cols(i)], T.wsc[:, cols(i)], T.z[:, 3 - i:3 - i + TILE]).then_inc(S.vw, 1)
-        g.wait_ge(S.vw, 4)
-        v = T.wq[:].bitcast(u8)
-        send(v, v, home, off, S.warr)
-        send(T.wsc[:], T.wsc[:], home, off, S.warr)
+        identity(0)
+        g.wait_ge(S["b%d" % r], len(_bits(chip_only)))
+        send(mycodes, mycodes, fourth, off, S["b%d" % r])
 
-    todo = ([r] if at_home else []) + jobs
-    if not at_home:
-        g.tensor.wait_ge(S.aarr, 3 * len(_bits(chip_only)))
+    if at_home:
+        todo = [r] + [(r + d) % NR for d in DIRECT]
+    else:
+        todo = [(r + RELAYED) % NR]
     for k, c in enumerate(todo):
         if c == r:
             g.tensor.wait_ge(S.vb, 1)
         else:
             g.tensor.wait_ge(S["b%d" % c], 2 * len(_bits(off)))
         for i in range(4):
-            if c == r and i % 2 == 0:
-                g.tensor.wait_ge(S.va, 1 + i // 2)
+            if k == 0 and i % 2 == 0:
+                if at_home:
+                    g.tensor.wait_ge(S.va, 1 + i // 2)
+                else:
+                    g.tensor.wait_ge(S["aarr%d" % (i // 2)], 2 * len(_bits(chip_only)))
             if k:
                 g.tensor.wait_ge(S.rs if i % 2 == 0 else S.rv, 2 * (k - 1) + 1 + i // 2)
-            g.tensor.matmul_mx(T.pt[:, 512 * i:512 * i + W], T.aq[:, cols(i)], T.asc[:, cols(i)],
-                               T.bq[:, cols(c)], T.bs[:, cols(c)], True, True).then_inc(S.mm, 1)
+            g.tensor.matmul_mx(T.pt[:, 512 * i:512 * i + W], T.bq[:, cols(c)], T.bs[:, cols(c)],
+                               T.aq[:, cols(i)], T.asc[:, cols(i)], True, True).then_inc(S.mm, 1)
         for i in range(4):
             o = T.h[:, c * TILE + i:(c + 1) * TILE:4]
             p = T.pt[:, 512 * i:512 * i + W]
@@ -141,8 +151,8 @@ def rank_program(g, core, T, topo):
             send(T.ts[:, cols(r)], T.hs[:, cols(c)], T.cores[c], off, S["t%d" % r])
 
     if at_home:
-        order = [r] + [(r - d) % NR for wave in WAVES for d in wave]
-        g.tensor.wait_ge(S.warr, 2 * len(_bits(off)))
+        order = [r] + [(r - d) % NR for d in DIRECT + (RELAYED,)]
+        g.tensor.wait_ge(S.warr, 4 * len(_bits(off)))
         for k, s in enumerate(order):
             if s == r:
                 g.tensor.wait_ge(S.vh, 1)
@@ -151,20 +161,21 @@ def rank_program(g, core, T, topo):
                 g.tensor.wait_ge(S["t%d" % s], 2 * len(_bits(off)))
                 x, xs = T.tq[:, cols(s)], T.ts[:, cols(s)]
             last = k == NR - 1
-            for i in range(4):
-                m = g.tensor.matmul_mx(T.py[:, 512 * i:512 * i + W], T.wq[:, cols(i)], T.wsc[:, cols(i)], x, xs, k == 0, last)
+            for j in range(4):
+                m = g.tensor.matmul_mx(T.py[:, 512 * j:512 * j + W], x, xs, T.wq[:, cols(j)], T.wsc[:, cols(j)], k == 0, last)
                 if last:
                     m.then_inc(S.my, 1)
-        for i in range(4):
-            o, p = T.ysb[:, i:TILE:4], T.py[:, 512 * i:512 * i + W]
-            if i % 2 == 0:
-                g.scalar.wait_ge(S.my, i + 1)
+        for j in range(4):
+            o, p = T.ysb[:, cols(j)], T.py[:, 512 * j:512 * j + W]
+            if j % 2 == 0:
+                g.scalar.wait_ge(S.my, j + 1)
                 g.scalar.activation(o, p, ActivationFunctionType.Copy).then_inc(S.ys, 1)
             else:
-                g.vector.wait_ge(S.my, i + 1)
+                g.vector.wait_ge(S.my, j + 1)
                 g.vector.tensor_copy(o, p).then_inc(S.yv, 1)
-        g.sync.wait_ge(S.ys, 2)
-        g.sync.wait_ge(S.yv, 2)
-        g.sync.dma_start(T.y[:], T.ysb[:]).then_inc(S.stored, 16)
-        g.sync.wait_ge(S.stored, 16)
+        for k, q in enumerate((g.sync, g.scalar)):
+            q.wait_ge(S.ys, k + 1)
+            q.wait_ge(S.yv, k + 1)
+            q.dma_start(T.y[:, cols(2 * k, 2)], T.ysb[:, cols(2 * k, 2)]).then_inc(S["st%d" % k], 16)
+            q.wait_ge(S["st%d" % k], 16)
     g.wait_ge(S.sent, sent[0])

@@ -4,7 +4,8 @@ from concourse.mybir import dt, AluOpType, ActivationFunctionType
 NR = 5
 W = 128
 TILE = 4 * W
-HALF = 2 * TILE
+PIECE = 4
+HOME, RELAY, HELPER = range(3)
 DIRECT, RELAYED = (1, 2, 3), 4
 
 SCRATCH = {
@@ -14,45 +15,50 @@ SCRATCH = {
     "bs": ("sbuf", [128, NR * W], "uint8"),
     "aq": ("sbuf", [128, 4 * W], "float8_e4m3fn_x4"),
     "asc": ("sbuf", [128, 4 * W], "uint8"),
+    "own": ("sbuf", [128, TILE], "float32"),
     "h": ("sbuf", [128, NR * TILE], "bfloat16"),
     "hq": ("sbuf", [128, NR * W], "float8_e4m3fn_x4"),
     "hs": ("sbuf", [128, NR * W], "uint8"),
     "tq": ("sbuf", [128, NR * W], "float8_e4m3fn_x4"),
     "ts": ("sbuf", [128, NR * W], "uint8"),
-    "z": ("sbuf", [128, HALF], "bfloat16"),
+    "z": ("sbuf", [128, 2 * TILE], "bfloat16"),
+    "eq": ("sbuf", [128, W], "float8_e4m3fn_x4"),
+    "es": ("sbuf", [128, W], "uint8"),
     "wq": ("sbuf", [128, 4 * W], "float8_e4m3fn_x4"),
     "wsc": ("sbuf", [128, 4 * W], "uint8"),
     "ysb": ("sbuf", [128, TILE], "float32"),
     "pt": ("psum", [128, 2048], "float32"),
     "py": ("psum", [128, 2048], "float32"),
 }
-SEMAPHORES = (["ldb", "lda0", "lda1", "vb", "va", "mm", "rs", "rv", "vh", "my", "ys", "yv", "st0", "st1", "sent", "aarr0",
-               "aarr1", "warr", "vm", "gz", "vw"] + ["b%d" % i for i in range(NR)] + ["t%d" % i for i in range(NR)])
+SEMAPHORES = (["ldb", "lda0", "lda1", "vb", "va", "mm", "rs", "rv", "vh", "my", "yv", "st0", "st1", "st2", "st3", "sent", "aarr0",
+               "aarr1", "warr", "vm0", "vm1", "gz", "vw"] + ["b%d" % i for i in range(NR)] + ["t%d" % i for i in range(NR)])
 
 
 def _bits(mask):
     return [e for e in range(16) if mask >> e & 1]
 
 
-def _workers(T, topo, r):
+def _crew(T, topo, r):
     home = T.cores[r]
     far = [c for c in range(max(0, home - 8), home + 9)
            if topo.host(c) == topo.host(home) and topo.chip(c) == topo.chip(home) and topo.die(c) != topo.die(home)]
-    return [home, far[-1], far[0]]
+    return [home, far[0], far[-1]]
 
 
 def rank_program(g, core, T, topo):
     S = T.sem
     u8 = dt.uint8
-    crew = [_workers(T, topo, r) for r in range(NR)]
+    crew = [_crew(T, topo, r) for r in range(NR)]
     mine = [r for r in range(NR) if core in crew[r]]
     if not mine:
         return
     r = mine[0]
-    home, helper, maker = crew[r]
-    at_home = core == home
-    off = topo.mask(core, T.cores[(r + 1) % NR])
-    chip_only = topo.mask(core, helper if at_home else home) & ~off
+    role = crew[r].index(core)
+    home, relay, helper = crew[r]
+    nxt = T.cores[(r + 1) % NR]
+    off = topo.mask(core, nxt)
+    chip_only = topo.mask(core, helper if role == HOME else home) & ~off
+    n_off, n_chip = len(_bits(off)), len(_bits(chip_only))
 
     def cols(k, n=1):
         return slice(k * W, (k + n) * W)
@@ -64,32 +70,24 @@ def rank_program(g, core, T, topo):
         g.remote_dma(out, view, sem, S.sent, pid, rid, mask)
         sent[0] += len(_bits(mask))
 
-    def identity(half):
-        p = slice(64 * half, 64 * half + 64)
-        g.vector.memset(T.z[:], 0.0).then_inc(S.vm, 1)
-        g.wait_ge(S.vm, 1)
-        for t in range(4):
-            v = T.z[p, 5 * t:HALF:16]
-            g.affine_select(v, v, [[1, 64]], AluOpType.not_equal, 1.0, 0, -1).then_inc(S.gz, 1)
-        g.vector.wait_ge(S.gz, 4)
-        w = cols(2 * half, 2)
-        g.vector.quantize_mx(T.wq[:, w], T.wsc[:, w], T.z[:]).then_inc(S.vw, 1)
-        g.wait_ge(S.vw, 1)
-        send(T.wq[:, w].bitcast(u8), T.wq[:, w].bitcast(u8), home, off, S.warr)
-        send(T.wsc[:, w], T.wsc[:, w], home, off, S.warr)
+    mycodes, myscales, bsem = T.bq[:, cols(r)].bitcast(u8), T.bs[:, cols(r)], S["b%d" % r]
+    fourth = crew[(r - RELAYED) % NR][HELPER]
 
-    if core == maker:
-        identity(1)
-        g.wait_ge(S.sent, sent[0])
-        return
-
-    mycodes, myscales = T.bq[:, cols(r)].bitcast(u8), T.bs[:, cols(r)]
-    fourth = crew[(r - RELAYED) % NR][1]
-    if at_home:
+    if role == HOME:
         g.sync.dma_start(T.bt[:], T.b[:]).then_inc(S.ldb, 16)
         for k in range(2):
             p = slice(k * 2 * TILE, (k + 1) * 2 * TILE)
             g.sync.dma_start(T.at[:, p], T.a[:, p]).then_inc(S["lda%d" % k], 16)
+        w = slice(0, PIECE)
+        g.vector.memset(T.z[:, 0:4 * PIECE], 0.0).then_inc(S.vm0, 1)
+        g.vector.memset(T.z[:, 4 * PIECE:TILE], 0.0).then_inc(S.vm1, 1)
+        g.vector.wait_ge(S.vm0, 1)
+        g.vector.memset(T.z[0:1, 0:4 * PIECE:5], 1.0).then_inc(S.vm1, 1)
+        g.vector.wait_ge(S.vm1, 2)
+        g.vector.quantize_mx(T.eq[:], T.es[:], T.z[:, 0:TILE]).then_inc(S.vw, 1)
+        g.wait_ge(S.vw, 1)
+        send(T.wq[:, w].bitcast(u8), T.eq[:, w].bitcast(u8), nxt, off, S.warr)
+
         g.vector.wait_ge(S.ldb, 16)
         g.vector.quantize_mx(T.bq[:, cols(r)], T.bs[:, cols(r)], T.bt[:]).then_inc(S.vb, 1)
         for k in range(2):
@@ -98,43 +96,56 @@ def rank_program(g, core, T, topo):
                                  T.at[:, k * 2 * TILE:(k + 1) * 2 * TILE]).then_inc(S.va, 1)
         g.wait_ge(S.vb, 1)
         for k, d in enumerate(DIRECT):
-            send(mycodes, mycodes, T.cores[(r - d) % NR], off, S["b%d" % r])
+            send(mycodes, mycodes, T.cores[(r - d) % NR], off, bsem)
+            send(myscales, myscales, T.cores[(r - d) % NR], off, bsem)
             if k == 0:
-                send(mycodes, mycodes, helper, chip_only, S["b%d" % r])
-            send(myscales, myscales, T.cores[(r - d) % NR], off, S["b%d" % r])
-        send(myscales, myscales, fourth, off, S["b%d" % r])
+                send(mycodes, mycodes, relay, chip_only, bsem)
+                send(myscales, myscales, relay, chip_only, bsem)
         for k in range(2):
             g.wait_ge(S.va, k + 1)
-            v = T.aq[:, cols(2 * k, 2)].bitcast(u8)
-            send(v, v, helper, chip_only, S["aarr%d" % k])
-            v = T.asc[:, cols(2 * k, 2)]
-            send(v, v, helper, chip_only, S["aarr%d" % k])
+            for v in (T.aq[:, cols(2 * k, 2)].bitcast(u8), T.asc[:, cols(2 * k, 2)]):
+                send(v, v, helper, chip_only, S["aarr%d" % k])
+        send(T.wsc[:, w], T.es[:, w], nxt, off, S.warr)
     else:
-        identity(0)
-        g.wait_ge(S["b%d" % r], len(_bits(chip_only)))
-        send(mycodes, mycodes, fourth, off, S["b%d" % r])
+        half = role - RELAY
+        p = slice(64 * half, 64 * half + 64)
+        g.vector.memset(T.z[:], 0.0).then_inc(S.vm0, 1)
+        g.wait_ge(S.vm0, 1)
+        for t in range(4):
+            v = T.z[p, 5 * t:2 * TILE:16]
+            g.affine_select(v, v, [[1, 64]], AluOpType.not_equal, 1.0, 0, -1).then_inc(S.gz, 1)
+        g.vector.wait_ge(S.gz, 4)
+        g.vector.quantize_mx(T.wq[:, cols(2 * half, 2)], T.wsc[:, cols(2 * half, 2)], T.z[:]).then_inc(S.vw, 1)
+        g.wait_ge(S.vw, 1)
+        w = slice(max(PIECE, 2 * W * half), 2 * W * (half + 1))
+        send(T.wsc[:, w], T.wsc[:, w], home, off, S.warr)
+        send(T.wq[:, w].bitcast(u8), T.wq[:, w].bitcast(u8), home, chip_only, S.warr)
+        if role == RELAY:
+            g.wait_ge(bsem, 2 * n_chip)
+            send(mycodes, mycodes, fourth, off, bsem)
+            send(myscales, myscales, fourth, off, bsem)
 
-    if at_home:
-        todo = [r] + [(r + d) % NR for d in DIRECT]
-    else:
-        todo = [(r + RELAYED) % NR]
+    todo = {HOME: [r] + [(r + d) % NR for d in DIRECT], RELAY: [], HELPER: [(r + RELAYED) % NR]}[role]
     for k, c in enumerate(todo):
-        if c == r:
+        owned = c == r
+        if owned:
             g.tensor.wait_ge(S.vb, 1)
         else:
-            g.tensor.wait_ge(S["b%d" % c], 2 * len(_bits(off)))
+            g.tensor.wait_ge(S["b%d" % c], 2 * n_off)
         for i in range(4):
             if k == 0 and i % 2 == 0:
-                if at_home:
+                if role == HOME:
                     g.tensor.wait_ge(S.va, 1 + i // 2)
                 else:
-                    g.tensor.wait_ge(S["aarr%d" % (i // 2)], 2 * len(_bits(chip_only)))
+                    g.tensor.wait_ge(S["aarr%d" % (i // 2)], 2 * n_chip)
             if k:
                 g.tensor.wait_ge(S.rs if i % 2 == 0 else S.rv, 2 * (k - 1) + 1 + i // 2)
-            g.tensor.matmul_mx(T.pt[:, 512 * i:512 * i + W], T.bq[:, cols(c)], T.bs[:, cols(c)],
-                               T.aq[:, cols(i)], T.asc[:, cols(i)], True, True).then_inc(S.mm, 1)
+            x = (T.bq[:, cols(c)], T.bs[:, cols(c)])
+            w = (T.aq[:, cols(i)], T.asc[:, cols(i)])
+            left, right = (w, x) if owned else (x, w)
+            g.tensor.matmul_mx(T.pt[:, 512 * i:512 * i + W], left[0], left[1], right[0], right[1], True, True).then_inc(S.mm, 1)
         for i in range(4):
-            o = T.h[:, c * TILE + i:(c + 1) * TILE:4]
+            o = T.own[:, i:TILE:4] if owned else T.h[:, c * TILE + i:(c + 1) * TILE:4]
             p = T.pt[:, 512 * i:512 * i + W]
             q = g.scalar if i % 2 == 0 else g.vector
             q.wait_ge(S.mm, 4 * k + i + 1)
@@ -142,40 +153,36 @@ def rank_program(g, core, T, topo):
                 g.scalar.activation(o, p, ActivationFunctionType.Relu).then_inc(S.rs, 1)
             else:
                 g.vector.tensor_scalar(o, p, 0.0, None, AluOpType.max).then_inc(S.rv, 1)
+        if owned:
+            continue
         g.vector.wait_ge(S.rs, 2 * (k + 1))
         g.vector.wait_ge(S.rv, 2 * (k + 1))
         g.vector.quantize_mx(T.hq[:, cols(c)], T.hs[:, cols(c)], T.h[:, c * TILE:(c + 1) * TILE]).then_inc(S.vh, 1)
-        if c != r:
-            g.wait_ge(S.vh, k + 1)
-            send(T.tq[:, cols(r)].bitcast(u8), T.hq[:, cols(c)].bitcast(u8), T.cores[c], off, S["t%d" % r])
-            send(T.ts[:, cols(r)], T.hs[:, cols(c)], T.cores[c], off, S["t%d" % r])
+        g.wait_ge(S.vh, k if role == HOME else k + 1)
+        send(T.tq[:, cols(r)].bitcast(u8), T.hq[:, cols(c)].bitcast(u8), T.cores[c], off, S["t%d" % r])
+        send(T.ts[:, cols(r)], T.hs[:, cols(c)], T.cores[c], off, S["t%d" % r])
 
-    if at_home:
-        order = [r] + [(r - d) % NR for d in DIRECT + (RELAYED,)]
-        g.tensor.wait_ge(S.warr, 4 * len(_bits(off)))
+    if role == HOME:
+        order = [(r - d) % NR for d in DIRECT + (RELAYED,)]
+        g.tensor.wait_ge(S.warr, 4 * n_off + 2 * n_chip)
         for k, s in enumerate(order):
-            if s == r:
-                g.tensor.wait_ge(S.vh, 1)
-                x, xs = T.hq[:, cols(r)], T.hs[:, cols(r)]
-            else:
-                g.tensor.wait_ge(S["t%d" % s], 2 * len(_bits(off)))
-                x, xs = T.tq[:, cols(s)], T.ts[:, cols(s)]
-            last = k == NR - 1
+            g.tensor.wait_ge(S["t%d" % s], 2 * n_off)
+            last = k == len(order) - 1
             for j in range(4):
-                m = g.tensor.matmul_mx(T.py[:, 512 * j:512 * j + W], x, xs, T.wq[:, cols(j)], T.wsc[:, cols(j)], k == 0, last)
+                m = g.tensor.matmul_mx(T.py[:, 512 * j:512 * j + W], T.tq[:, cols(s)], T.ts[:, cols(s)],
+                                       T.wq[:, cols(j)], T.wsc[:, cols(j)], k == 0, last)
                 if last:
                     m.then_inc(S.my, 1)
+        g.vector.wait_ge(S.rs, 2)
+        g.vector.wait_ge(S.rv, 2)
         for j in range(4):
-            o, p = T.ysb[:, cols(j)], T.py[:, 512 * j:512 * j + W]
-            if j % 2 == 0:
-                g.scalar.wait_ge(S.my, j + 1)
-                g.scalar.activation(o, p, ActivationFunctionType.Copy).then_inc(S.ys, 1)
-            else:
-                g.vector.wait_ge(S.my, j + 1)
-                g.vector.tensor_copy(o, p).then_inc(S.yv, 1)
-        for k, q in enumerate((g.sync, g.scalar)):
-            q.wait_ge(S.ys, k + 1)
-            q.wait_ge(S.yv, k + 1)
-            q.dma_start(T.y[:, cols(2 * k, 2)], T.ysb[:, cols(2 * k, 2)]).then_inc(S["st%d" % k], 16)
-            q.wait_ge(S["st%d" % k], 16)
+            g.vector.wait_ge(S.my, j + 1)
+            g.vector.tensor_tensor(T.ysb[:, cols(j)], T.py[:, 512 * j:512 * j + W], T.own[:, cols(j)], AluOpType.add).then_inc(S.yv, 1)
+        for j in range(4):
+            q = g.sync if j % 2 == 0 else g.scalar
+            q.wait_ge(S.yv, j + 1)
+            q.dma_start(T.y[:, cols(j)], T.ysb[:, cols(j)]).then_inc(S["st%d" % j], 16)
+        for j in range(4):
+            q = g.sync if j % 2 == 0 else g.scalar
+            q.wait_ge(S["st%d" % j], 16)
     g.wait_ge(S.sent, sent[0])

from concourse.bass import DstId, RemoteDMATransfer
from concourse.mybir import dt, AluOpType, ActivationFunctionType

NR = 5
W = 128
TILE = 4 * W
PIECE = 4
HOME, RELAY, HELPER = range(3)
DIRECT, RELAYED = (1, 2, 3), 4

SCRATCH = {
    "bt": ("sbuf", [128, TILE], "bfloat16"),
    "at": ("sbuf", [128, 4 * TILE], "bfloat16"),
    "bq": ("sbuf", [128, NR * W], "float8_e4m3fn_x4"),
    "bs": ("sbuf", [128, NR * W], "uint8"),
    "aq": ("sbuf", [128, 4 * W], "float8_e4m3fn_x4"),
    "asc": ("sbuf", [128, 4 * W], "uint8"),
    "own": ("sbuf", [128, TILE], "float32"),
    "h": ("sbuf", [128, NR * TILE], "bfloat16"),
    "hq": ("sbuf", [128, NR * W], "float8_e4m3fn_x4"),
    "hs": ("sbuf", [128, NR * W], "uint8"),
    "tq": ("sbuf", [128, NR * W], "float8_e4m3fn_x4"),
    "ts": ("sbuf", [128, NR * W], "uint8"),
    "z": ("sbuf", [128, 2 * TILE], "bfloat16"),
    "eq": ("sbuf", [128, W], "float8_e4m3fn_x4"),
    "es": ("sbuf", [128, W], "uint8"),
    "wq": ("sbuf", [128, 4 * W], "float8_e4m3fn_x4"),
    "wsc": ("sbuf", [128, 4 * W], "uint8"),
    "ysb": ("sbuf", [128, TILE], "float32"),
    "pt": ("psum", [128, 2048], "float32"),
    "py": ("psum", [128, 2048], "float32"),
}
SEMAPHORES = (["ldb", "lda0", "lda1", "vb", "va", "mm", "rs", "rv", "vh", "my", "yv", "st0", "st1", "st2", "st3", "sent", "aarr0",
               "aarr1", "warr", "vm0", "vm1", "gz", "vw"] + ["b%d" % i for i in range(NR)] + ["t%d" % i for i in range(NR)])


def _bits(mask):
    return [e for e in range(16) if mask >> e & 1]


def _crew(T, topo, r):
    home = T.cores[r]
    far = [c for c in range(max(0, home - 8), home + 9)
           if topo.host(c) == topo.host(home) and topo.chip(c) == topo.chip(home) and topo.die(c) != topo.die(home)]
    return [home, far[0], far[-1]]


def rank_program(g, core, T, topo):
    S = T.sem
    u8 = dt.uint8
    crew = [_crew(T, topo, r) for r in range(NR)]
    mine = [r for r in range(NR) if core in crew[r]]
    if not mine:
        return
    r = mine[0]
    role = crew[r].index(core)
    home, relay, helper = crew[r]
    nxt = T.cores[(r + 1) % NR]
    off = topo.mask(core, nxt)
    chip_only = topo.mask(core, helper if role == HOME else home) & ~off
    n_off, n_chip = len(_bits(off)), len(_bits(chip_only))

    def cols(k, n=1):
        return slice(k * W, (k + n) * W)

    sent = [0]

    def send(out, view, to, mask, sem):
        rid, pid = topo.addr(to, core)
        g.remote_dma(out, view, sem, S.sent, pid, rid, mask)
        sent[0] += len(_bits(mask))

    mycodes, myscales, bsem = T.bq[:, cols(r)].bitcast(u8), T.bs[:, cols(r)], S["b%d" % r]
    fourth = crew[(r - RELAYED) % NR][HELPER]

    if role == HOME:
        g.sync.dma_start(T.bt[:], T.b[:]).then_inc(S.ldb, 16)
        for k in range(2):
            p = slice(k * 2 * TILE, (k + 1) * 2 * TILE)
            g.sync.dma_start(T.at[:, p], T.a[:, p]).then_inc(S["lda%d" % k], 16)
        w = slice(0, PIECE)
        g.vector.memset(T.z[:, 0:4 * PIECE], 0.0).then_inc(S.vm0, 1)
        g.vector.memset(T.z[:, 4 * PIECE:TILE], 0.0).then_inc(S.vm1, 1)
        g.vector.wait_ge(S.vm0, 1)
        g.vector.memset(T.z[0:1, 0:4 * PIECE:5], 1.0).then_inc(S.vm1, 1)
        g.vector.wait_ge(S.vm1, 2)
        g.vector.quantize_mx(T.eq[:], T.es[:], T.z[:, 0:TILE]).then_inc(S.vw, 1)
        g.wait_ge(S.vw, 1)
        send(T.wq[:, w].bitcast(u8), T.eq[:, w].bitcast(u8), nxt, off, S.warr)

        g.vector.wait_ge(S.ldb, 16)
        g.vector.quantize_mx(T.bq[:, cols(r)], T.bs[:, cols(r)], T.bt[:]).then_inc(S.vb, 1)
        for k in range(2):
            g.vector.wait_ge(S["lda%d" % k], 16)
            g.vector.quantize_mx(T.aq[:, cols(2 * k, 2)], T.asc[:, cols(2 * k, 2)],
                                 T.at[:, k * 2 * TILE:(k + 1) * 2 * TILE]).then_inc(S.va, 1)
        g.wait_ge(S.vb, 1)
        for k, d in enumerate(DIRECT):
            send(mycodes, mycodes, T.cores[(r - d) % NR], off, bsem)
            send(myscales, myscales, T.cores[(r - d) % NR], off, bsem)
            if k == 0:
                send(mycodes, mycodes, relay, chip_only, bsem)
                send(myscales, myscales, relay, chip_only, bsem)
        for k in range(2):
            g.wait_ge(S.va, k + 1)
            for v in (T.aq[:, cols(2 * k, 2)].bitcast(u8), T.asc[:, cols(2 * k, 2)]):
                send(v, v, helper, chip_only, S["aarr%d" % k])
        send(T.wsc[:, w], T.es[:, w], nxt, off, S.warr)
    else:
        half = role - RELAY
        p = slice(64 * half, 64 * half + 64)
        g.vector.memset(T.z[:], 0.0).then_inc(S.vm0, 1)
        g.wait_ge(S.vm0, 1)
        for t in range(4):
            v = T.z[p, 5 * t:2 * TILE:16]
            g.affine_select(v, v, [[1, 64]], AluOpType.not_equal, 1.0, 0, -1).then_inc(S.gz, 1)
        g.vector.wait_ge(S.gz, 4)
        g.vector.quantize_mx(T.wq[:, cols(2 * half, 2)], T.wsc[:, cols(2 * half, 2)], T.z[:]).then_inc(S.vw, 1)
        g.wait_ge(S.vw, 1)
        w = slice(max(PIECE, 2 * W * half), 2 * W * (half + 1))
        send(T.wsc[:, w], T.wsc[:, w], home, off, S.warr)
        send(T.wq[:, w].bitcast(u8), T.wq[:, w].bitcast(u8), home, chip_only, S.warr)
        if role == RELAY:
            g.wait_ge(bsem, 2 * n_chip)
            send(mycodes, mycodes, fourth, off, bsem)
            send(myscales, myscales, fourth, off, bsem)

    todo = {HOME: [r] + [(r + d) % NR for d in DIRECT], RELAY: [], HELPER: [(r + RELAYED) % NR]}[role]
    for k, c in enumerate(todo):
        owned = c == r
        if owned:
            g.tensor.wait_ge(S.vb, 1)
        else:
            g.tensor.wait_ge(S["b%d" % c], 2 * n_off)
        for i in range(4):
            if k == 0 and i % 2 == 0:
                if role == HOME:
                    g.tensor.wait_ge(S.va, 1 + i // 2)
                else:
                    g.tensor.wait_ge(S["aarr%d" % (i // 2)], 2 * n_chip)
            if k:
                g.tensor.wait_ge(S.rs if i % 2 == 0 else S.rv, 2 * (k - 1) + 1 + i // 2)
            x = (T.bq[:, cols(c)], T.bs[:, cols(c)])
            w = (T.aq[:, cols(i)], T.asc[:, cols(i)])
            left, right = (w, x) if owned else (x, w)
            g.tensor.matmul_mx(T.pt[:, 512 * i:512 * i + W], left[0], left[1], right[0], right[1], True, True).then_inc(S.mm, 1)
        for i in range(4):
            o = T.own[:, i:TILE:4] if owned else T.h[:, c * TILE + i:(c + 1) * TILE:4]
            p = T.pt[:, 512 * i:512 * i + W]
            q = g.scalar if i % 2 == 0 else g.vector
            q.wait_ge(S.mm, 4 * k + i + 1)
            if i % 2 == 0:
                g.scalar.activation(o, p, ActivationFunctionType.Relu).then_inc(S.rs, 1)
            else:
                g.vector.tensor_scalar(o, p, 0.0, None, AluOpType.max).then_inc(S.rv, 1)
        if owned:
            continue
        g.vector.wait_ge(S.rs, 2 * (k + 1))
        g.vector.wait_ge(S.rv, 2 * (k + 1))
        g.vector.quantize_mx(T.hq[:, cols(c)], T.hs[:, cols(c)], T.h[:, c * TILE:(c + 1) * TILE]).then_inc(S.vh, 1)
        g.wait_ge(S.vh, k if role == HOME else k + 1)
        send(T.tq[:, cols(r)].bitcast(u8), T.hq[:, cols(c)].bitcast(u8), T.cores[c], off, S["t%d" % r])
        send(T.ts[:, cols(r)], T.hs[:, cols(c)], T.cores[c], off, S["t%d" % r])

    if role == HOME:
        order = [(r - d) % NR for d in DIRECT + (RELAYED,)]
        g.tensor.wait_ge(S.warr, 4 * n_off + 2 * n_chip)
        for k, s in enumerate(order):
            g.tensor.wait_ge(S["t%d" % s], 2 * n_off)
            last = k == len(order) - 1
            for j in range(4):
                m = g.tensor.matmul_mx(T.py[:, 512 * j:512 * j + W], T.tq[:, cols(s)], T.ts[:, cols(s)],
                                       T.wq[:, cols(j)], T.wsc[:, cols(j)], k == 0, last)
                if last:
                    m.then_inc(S.my, 1)
        g.vector.wait_ge(S.rs, 2)
        g.vector.wait_ge(S.rv, 2)
        for j in range(4):
            g.vector.wait_ge(S.my, j + 1)
            g.vector.tensor_tensor(T.ysb[:, cols(j)], T.py[:, 512 * j:512 * j + W], T.own[:, cols(j)], AluOpType.add).then_inc(S.yv, 1)
        for j in range(4):
            q = g.sync if j % 2 == 0 else g.scalar
            q.wait_ge(S.yv, j + 1)
            q.dma_start(T.y[:, cols(j)], T.ysb[:, cols(j)]).then_inc(S["st%d" % j], 16)
        for j in range(4):
            q = g.sync if j % 2 == 0 else g.scalar
            q.wait_ge(S["st%d" % j], 16)
    g.wait_ge(S.sent, sent[0])
